import numpy as np
import ml_dtypes


def mxq(x, axis, fmt="e4m3"):
    dtype, down = {"e4m3": (ml_dtypes.float8_e4m3fn, 7), "e5m2": (ml_dtypes.float8_e5m2, 14)}[fmt]
    v = np.moveaxis(np.asarray(x, np.float32).astype(ml_dtypes.bfloat16).astype(np.float64), axis, -1)
    blocks = v.reshape(v.shape[:-1] + (-1, 32))
    amax = np.abs(blocks).max(-1, keepdims=True)
    byte = np.maximum(np.where(amax > 0, np.frexp(amax)[1] - 1 + 127, 0) - down, 1)
    scale = np.exp2(byte - 127.0)
    codes = (blocks / scale).astype(np.float32).astype(dtype).astype(np.float64)
    return np.moveaxis((codes * scale).reshape(v.shape), -1, axis)


WIDE = False


def mx_kscale(k):
    if not WIDE:
        return np.ones(k)
    levels = np.array([10, -10, 5, -5, 0])
    if k % 512:
        return np.exp2(np.random.permutation(np.resize(levels, k // 32))).repeat(32)
    a = np.empty((k // 512, 16))
    for p in range(k // 512):
        a[p, :8] = np.random.permutation(np.resize(levels, 8))
        for g in range(8):
            far = levels[np.abs(levels - a[p, g]) >= 10]
            a[p, g + 8] = far[np.random.randint(len(far))]
    return np.exp2(a.ravel()).repeat(32)


def f64(x):
    return np.asarray(x).astype(np.float64)


def striped(idx):
    return np.tile(idx.reshape(-1, 16).T, (8, 1)).astype(np.uint16)


def unstriped(offs):
    return offs[:16].T.reshape(-1).astype(np.int64)


def striped8(idx):
    return np.concatenate([x.reshape(-1, 16).T for x in idx]).astype(np.uint16)


def runs(offs, k):
    lists = np.stack([offs[16 * r : 16 * r + 16].T.reshape(-1) for r in range(8)]).astype(np.int64)
    return lists[np.arange(k) % 512 // 64]


def pack_weight(w):
    k, n = w.shape
    w = f64(np.asarray(w, np.float32).astype(ml_dtypes.bfloat16)).reshape(k // 32, 32, n)
    amax = np.abs(w).max(1)
    byte = np.clip(np.where(amax > 0, np.frexp(amax)[1] - 1 + 127 - 7, 1), 1, 254)
    scaled = (w * np.exp2(127.0 - byte)[:, None, :]).reshape(k, n).astype(np.float32)
    words = np.ascontiguousarray(scaled.reshape(k // 512, 128, 4, n).transpose(0, 1, 3, 2)).astype(ml_dtypes.float8_e4m3fn).view(np.uint8)
    return words, np.ascontiguousarray(byte.astype(np.uint8).reshape(k // 512, 16, n))


def unpack_weight(words, scales):
    g, p, n, _ = words.shape
    vals = np.ascontiguousarray(words).view(ml_dtypes.float8_e4m3fn).astype(np.float64) * np.repeat(np.exp2(scales.astype(np.float64) - 127.0), 8, axis=1)[..., None]
    return vals.transpose(0, 1, 3, 2).reshape(g * 512, n)


K, T, S, G, H, W, U = 512, 1024, 256, 2048, 512, 128, 512


def setup_inputs():
    n = np.random.standard_normal
    s = mx_kscale(K)[:, None]
    packed_xT = pack_weight(n((K, T)) * s)
    packed_dT = pack_weight(n((K, G)) / s)
    perm = np.random.permutation(S)
    perm2 = np.random.permutation(U)
    return {
        "x_words": packed_xT[0],
        "x_scales": packed_xT[1],
        "d_words": packed_dT[0],
        "d_scales": packed_dT[1],
        "gs": (np.random.uniform(0.5, 1.5, (K, 1)) * s).astype(np.float32),
        "offs": striped8(np.random.randint(0, T, (8, S))),
        "k1": striped8(np.random.randint(0, G, (8, H))),
        "n1": striped(perm[:W]),
        "n2": striped(perm[W:]),
        "n3": striped(np.random.permutation(S)),
        "k2": striped8(np.random.randint(0, G, (8, H))),
        "n4": striped(perm2[:S]),
        "n5": striped(perm2[S:]),
        "n6": striped(np.random.permutation(S)),
    }


def reference(x_words, x_scales, d_words, d_scales, gs, offs, k1, n1, n2, n3, k2, n4, n5, n6):
    d_k2 = unpack_weight(d_words, d_scales)[np.arange(K)[:, None], runs(k2, K)]
    d_k1 = unpack_weight(d_words, d_scales)[np.arange(K)[:, None], runs(k1, K)]
    xq = unpack_weight(x_words, x_scales)[np.arange(K)[:, None], runs(offs, K)]
    h = 0.0625 * (d_k1.T @ xq)
    pa = h[:, unstriped(n1)]
    pb = h[:, unstriped(n2)]
    rb = pa - pb
    ds = np.zeros((H, S))
    ds[:, unstriped(n1)] = pb
    dt = ds.copy()
    dt[:, unstriped(n2)] = rb
    z = f64(gs) * (np.maximum(dt, 0.5 * dt[:, unstriped(n3)]))
    h2 = 0.0625 * ((d_k2.T @ mxq(z, 0, "e4m3")))
    dn = np.minimum(h2, h2[:, unstriped(n6)])
    up = np.maximum(h2, h2[:, unstriped(n6)])
    ph = np.zeros((H, U))
    ph[:, unstriped(n4)] = up
    out = ph.copy()
    out[:, unstriped(n5)] = dn
    return out

@@ -1,0 +1,202 @@
+from contextlib import ExitStack
+
+import concourse.mybir as mybir
+
+K, T, S, G, H, W, U = 512, 1024, 256, 2048, 512, 128, 512
+FLOPS = 2 * 2 * K * H * S
+
+F32 = mybir.dt.float32
+BF16 = mybir.dt.bfloat16
+I32 = mybir.dt.int32
+U32 = mybir.dt.uint32
+U16 = mybir.dt.uint16
+U8 = mybir.dt.uint8
+FP8X4 = mybir.dt.float8_e4m3fn_x4
+ALU = mybir.AluOpType
+COPY = mybir.ActivationFunctionType.Copy
+
+P = 128
+PACK = 4
+HALF = S // 2
+SPARE = 16
+
+
+def tile_picked_hcodeswapdpagmx_none_p_kernel(
+    tc, x_words, x_scales, d_words, d_scales, gs, offs, k1, n1, n2, n3, k2, n4, n5, n6, out
+):
+    nc = tc.nc
+    with ExitStack() as ctx:
+        lists = ctx.enter_context(tc.tile_pool(name="lists", bufs=1))
+        keep = ctx.enter_context(tc.tile_pool(name="keep", bufs=1))
+        psum = ctx.enter_context(tc.psum_pool(name="psum", bufs=1))
+
+        def load_list(name, src):
+            held = lists.tile(list(src.shape), U16, name=name)
+            nc.sync.dma_start(held[:], src)
+            return held
+
+        def load_scale_rows(name, src, width, clear):
+            window = keep.tile([P, width], U8, name=name, align_bytes=64)
+            clear.memset(window[:].bitcast(I32), 0)
+            nc.sync.dma_start(window[0:P:8, :].bitcast(I32), src[0].bitcast(I32))
+            return window
+
+        def load_words(name, src, width):
+            window = keep.tile([P, width], U32, name=name, align_bytes=64)
+            nc.sync.dma_start(window[:].bitcast(I32), src[0].rearrange("p n r -> p (n r)").bitcast(I32))
+            return window
+
+        def place_scale_rows(plane, queue):
+            for a in range(1, 4):
+                queue.dma_start(plane[a:P:32, :].bitcast(I32), plane[8 * a : P : 32, :].bitcast(I32))
+
+        k1_l = load_list("k1_l", k1)
+        offs_l = load_list("offs_l", offs)
+        d_sc = load_scale_rows("d_sc", d_scales, G, nc.gpsimd)
+        x_sc = load_scale_rows("x_sc", x_scales, T, nc.vector)
+        d_w = load_words("d_w", d_words, G)
+        n2_l = load_list("n2_l", n2)
+        n1_l = load_list("n1_l", n1)
+        n3_l = load_list("n3_l", n3)
+        gain = keep.tile([P, PACK], F32, name="gain")
+        nc.sync.dma_start(gain[:], gs.rearrange("(p t) o -> p (t o)", t=PACK))
+        x_w = load_words("x_w", x_words, T)
+        k2_l = load_list("k2_l", k2)
+        n6_l = load_list("n6_l", n6)
+        n4_l = load_list("n4_l", n4)
+        n5_l = load_list("n5_l", n5)
+
+        plane1 = keep.tile([P, H + S], U8, name="plane1", align_bytes=64)
+        w1_bytes = keep.tile([P, H], U8, name="w1_bytes", align_bytes=64)
+        nc.vector.tensor_copy(w1_bytes[:], d_sc[:].indirect(k1_l[:]))
+        nc.vector.tensor_copy(
+            plane1[:, 0:H].rearrange("p (t m) -> p t m", t=PACK), w1_bytes[:].rearrange("p (m t) -> p t m", t=PACK)
+        )
+        xq_bytes = keep.tile([P, S], U8, name="xq_bytes", align_bytes=64)
+        nc.vector.tensor_copy(xq_bytes[:], x_sc[:].indirect(offs_l[:]))
+        nc.vector.tensor_copy(plane1[:, H:].bitcast(I32), xq_bytes[:].bitcast(I32))
+        place_scale_rows(plane1, nc.scalar)
+
+        w1_picked = keep.tile([P, H], U32, name="w1_picked", align_bytes=64)
+        nc.vector.tensor_copy(w1_picked[:], d_w[:].indirect(k1_l[:]))
+        xq = keep.tile([P, S], U32, name="xq", align_bytes=64)
+        nc.vector.tensor_copy(xq[:], x_w[:].indirect(offs_l[:]))
+
+        h = []
+        for t in range(PACK):
+            w1 = keep.tile([P, P], U32, name=f"w1_{t}", align_bytes=64)
+            nc.vector.tensor_copy(w1[:], w1_picked[:, t:H:PACK])
+            acc = psum.tile([P, S], F32, name=f"acc1_{t}", tag=f"bank{t}")
+            nc.tensor.matmul_mx(
+                out=acc[:], lhsT=w1[:].bitcast(FP8X4), lhsT_scale=plane1[:, P * t : P * (t + 1)],
+                rhs=xq[:].bitcast(FP8X4), rhs_scale=plane1[:, H : H + S], start=True, stop=True,
+            )
+            h_t = keep.tile([P, S], F32, name=f"h{t}")
+            nc.vector.tensor_scalar(h_t[:], acc[:], 0.0625, None, ALU.mult)
+            h.append(h_t)
+
+        pa = [keep.tile([P, W], F32, name=f"pa{t}", tag=f"after_pairs{t}", align_bytes=64) for t in range(PACK)]
+        pb = [keep.tile([P, W], F32, name=f"pb{t}") for t in range(PACK)]
+        rb = [keep.tile([P, W], F32, name=f"rb{t}") for t in range(PACK)]
+        dt = [keep.tile([P, S + (SPARE if t + 1 < PACK else 0)], F32, name=f"dt{t}") for t in range(PACK)]
+        h2 = [keep.tile([P, S + SPARE], F32, name=f"h2_{u}") for u in range(PACK)]
+        for window in dt[:-1] + h2:
+            nc.vector.memset(window[:, S:], 0.0)
+        z = [keep.tile([P, HALF, PACK], BF16, name=f"z{c}", align_bytes=64) for c in range(2)]
+
+        def fetch_pairs(t):
+            nc.scalar.activation(pb[t][:], h[t][:].indirect(n2_l[:]), COPY)
+            nc.scalar.activation(pa[t][:], h[t][:].indirect(n1_l[:]), COPY)
+            nc.vector.tensor_tensor(rb[t][:], pa[t][:], pb[t][:], ALU.subtract)
+
+        def weigh(t, c, far):
+            top = keep.tile([P, HALF], F32, name=f"top{t}_{c}")
+            nc.vector.scalar_tensor_tensor(
+                top[:], far, 0.5, dt[t][:, HALF * c : HALF * (c + 1)], ALU.mult, ALU.max
+            )
+            nc.vector.tensor_scalar(z[c][:, :, t], top[:], gain[:, t : t + 1], None, ALU.mult)
+
+        def fetch_partners(t):
+            far = keep.tile([P, S], F32, name=f"far{t}")
+            nc.scalar.activation(far[:], dt[t][:].indirect(n3_l[:]), COPY)
+            for c in range(2):
+                weigh(t, c, far[:, HALF * c : HALF * (c + 1)])
+
+        def fetch_half_partners(t, c):
+            far = keep.tile([P, HALF], F32, name=f"far{t}_{c}")
+            nc.scalar.activation(far[:], dt[t][:].indirect(n3_l[:, 8 * c : 8 * c + 8]), COPY)
+            weigh(t, c, far[:])
+
+        fetch_pairs(0)
+        for t in range(PACK):
+            nc.scalar.activation(dt[t][:].indirect(n1_l[:]), pb[t][:], COPY)
+            if t > 0:
+                fetch_partners(t - 1)
+            nc.scalar.activation(dt[t][:].indirect(n2_l[:]), rb[t][:], COPY)
+            if t + 1 < PACK:
+                fetch_pairs(t + 1)
+            if t == 0:
+                w2_bytes = keep.tile([P, H], U8, name="w2_bytes", tag="after_pairs0", align_bytes=64)
+                nc.vector.tensor_copy(w2_bytes[:], d_sc[:].indirect(k2_l[:]))
+                plane2 = keep.tile([P, H], U8, name="plane2", align_bytes=64)
+                nc.vector.tensor_copy(plane2[:].bitcast(I32), w2_bytes[:].bitcast(I32))
+                place_scale_rows(plane2, nc.sync)
+            if t == 1:
+                w2 = keep.tile([P, H], U32, name="w2", tag="after_pairs1", align_bytes=64)
+                nc.vector.tensor_copy(w2[:], d_w[:].indirect(k2_l[:]))
+
+        zq = keep.tile([P, S], U32, name="zq", align_bytes=64)
+        zq_sc = keep.tile([P, S], U8, name="zq_sc", align_bytes=64)
+        nc.vector.memset(zq_sc[:].bitcast(I32), 0)
+
+        def second_product(u, cols, bank, copy_on_scalar):
+            acc = psum.tile([P, cols.stop - cols.start], F32, name=f"acc2_{bank}", tag=f"bank{bank}")
+            nc.tensor.matmul_mx(
+                out=acc[:], lhsT=w2[:, P * u : P * (u + 1)].bitcast(FP8X4),
+                lhsT_scale=plane2[:, P * u : P * (u + 1)],
+                rhs=zq[:, cols].bitcast(FP8X4), rhs_scale=zq_sc[:, cols], start=True, stop=True,
+            )
+            if copy_on_scalar:
+                nc.scalar.activation(h2[u][:, cols], acc[:], COPY, scale=0.0625)
+            else:
+                nc.vector.tensor_scalar(h2[u][:, cols], acc[:], 0.0625, None, ALU.mult)
+
+        for c in range(2):
+            cols = slice(HALF * c, HALF * (c + 1))
+            fetch_half_partners(PACK - 1, c)
+            nc.vector.quantize_mx(
+                out=zq[:, cols].bitcast(FP8X4), scales=zq_sc[:, cols], in_=z[c][:].rearrange("p j t -> p (j t)")
+            )
+            second_product(0, cols, 4 + c, c == 0)
+        for u in range(1, PACK):
+            second_product(u, slice(0, S), u, False)
+
+        up = [keep.tile([P, S], F32, name=f"up{u}") for u in range(PACK)]
+        dn = [keep.tile([P, S], F32, name=f"dn{u}") for u in range(PACK)]
+        page = [keep.tile([P, U], F32, name=f"page{u}") for u in range(PACK)]
+
+        def sort_pairs(u):
+            mate = keep.tile([P, S], F32, name=f"mate{u}")
+            nc.scalar.activation(mate[:], h2[u][:].indirect(n6_l[:]), COPY)
+            nc.vector.tensor_tensor(up[u][:], h2[u][:, 0:S], mate[:], ALU.max)
+            nc.vector.tensor_tensor(dn[u][:], h2[u][:, 0:S], mate[:], ALU.min)
+
+        def put_up(u):
+            nc.scalar.activation(page[u][:].indirect(n4_l[:]), up[u][:], COPY)
+
+        def put_down(u):
+            nc.scalar.activation(page[u][:].indirect(n5_l[:]), dn[u][:], COPY)
+            nc.sync.dma_start(out[P * u : P * (u + 1), :], page[u][:])
+
+        sort_pairs(0)
+        sort_pairs(1)
+        put_up(0)
+        sort_pairs(2)
+        put_down(0)
+        put_up(1)
+        sort_pairs(3)
+        put_down(1)
+        put_up(2)
+        put_up(3)
+        put_down(2)
+        put_down(3)

@@ -46,8 +46,8 @@ def tile_picked_hcodeswapdpagmx_none_p_kernel(
             nc.sync.dma_start(window[:].bitcast(I32), src[0].rearrange("p n r -> p (n r)").bitcast(I32))
             return window
 
-        def place_scale_rows(plane, queue):
-            for a in range(1, 4):
+        def place_scale_rows(plane, queues):
+            for a, queue in zip(range(1, 4), queues):
                 queue.dma_start(plane[a:P:32, :].bitcast(I32), plane[8 * a : P : 32, :].bitcast(I32))
 
         k1_l = load_list("k1_l", k1)
@@ -58,8 +58,6 @@ def tile_picked_hcodeswapdpagmx_none_p_kernel(
         n2_l = load_list("n2_l", n2)
         n1_l = load_list("n1_l", n1)
         n3_l = load_list("n3_l", n3)
-        gain = keep.tile([P, PACK], F32, name="gain")
-        nc.sync.dma_start(gain[:], gs.rearrange("(p t) o -> p (t o)", t=PACK))
         x_w = load_words("x_w", x_words, T)
         k2_l = load_list("k2_l", k2)
         n6_l = load_list("n6_l", n6)
@@ -75,9 +73,9 @@ def tile_picked_hcodeswapdpagmx_none_p_kernel(
         xq_bytes = keep.tile([P, S], U8, name="xq_bytes", align_bytes=64)
         nc.vector.tensor_copy(xq_bytes[:], x_sc[:].indirect(offs_l[:]))
         nc.vector.tensor_copy(plane1[:, H:].bitcast(I32), xq_bytes[:].bitcast(I32))
-        place_scale_rows(plane1, nc.scalar)
+        place_scale_rows(plane1, (nc.scalar, nc.scalar, nc.scalar))
 
-        w1_picked = keep.tile([P, H], U32, name="w1_picked", align_bytes=64)
+        w1_picked = keep.tile([P, H], U32, name="w1_picked", tag="after_deal", align_bytes=64)
         nc.vector.tensor_copy(w1_picked[:], d_w[:].indirect(k1_l[:]))
         xq = keep.tile([P, S], U32, name="xq", align_bytes=64)
         nc.vector.tensor_copy(xq[:], x_w[:].indirect(offs_l[:]))
@@ -86,21 +84,29 @@ def tile_picked_hcodeswapdpagmx_none_p_kernel(
         for t in range(PACK):
             w1 = keep.tile([P, P], U32, name=f"w1_{t}", align_bytes=64)
             nc.vector.tensor_copy(w1[:], w1_picked[:, t:H:PACK])
-            acc = psum.tile([P, S], F32, name=f"acc1_{t}", tag=f"bank{t}")
-            nc.tensor.matmul_mx(
-                out=acc[:], lhsT=w1[:].bitcast(FP8X4), lhsT_scale=plane1[:, P * t : P * (t + 1)],
-                rhs=xq[:].bitcast(FP8X4), rhs_scale=plane1[:, H : H + S], start=True, stop=True,
-            )
             h_t = keep.tile([P, S], F32, name=f"h{t}")
-            nc.vector.tensor_scalar(h_t[:], acc[:], 0.0625, None, ALU.mult)
+            parts = [(slice(0, HALF), 4), (slice(HALF, S), 0)] if t == 0 else [(slice(0, S), t)]
+            for cols, bank in parts:
+                acc = psum.tile([P, cols.stop - cols.start], F32, name=f"acc1_{bank}", tag=f"bank{bank}")
+                nc.tensor.matmul_mx(
+                    out=acc[:], lhsT=w1[:].bitcast(FP8X4), lhsT_scale=plane1[:, P * t : P * (t + 1)],
+                    rhs=xq[:, cols].bitcast(FP8X4), rhs_scale=plane1[:, H + cols.start : H + cols.stop],
+                    start=True, stop=True,
+                )
+                if bank == 4:
+                    nc.scalar.activation(h_t[:, cols], acc[:], COPY, scale=0.0625)
+                else:
+                    nc.vector.tensor_scalar(h_t[:, cols], acc[:], 0.0625, None, ALU.mult)
             h.append(h_t)
 
+        gain = keep.tile([P, PACK], F32, name="gain", tag="after_deal", align_bytes=64)
+        nc.sync.dma_start(gain[:], gs.rearrange("k o -> (k o)").rearrange("(p t) -> p t", t=PACK))
         pa = [keep.tile([P, W], F32, name=f"pa{t}", tag=f"after_pairs{t}", align_bytes=64) for t in range(PACK)]
         pb = [keep.tile([P, W], F32, name=f"pb{t}") for t in range(PACK)]
         rb = [keep.tile([P, W], F32, name=f"rb{t}") for t in range(PACK)]
-        dt = [keep.tile([P, S + (SPARE if t + 1 < PACK else 0)], F32, name=f"dt{t}") for t in range(PACK)]
+        dt = [keep.tile([P, S + (SPARE if t < 3 else 0)], F32, name=f"dt{t}") for t in range(PACK)]
         h2 = [keep.tile([P, S + SPARE], F32, name=f"h2_{u}") for u in range(PACK)]
-        for window in dt[:-1] + h2:
+        for window in dt[:3] + h2:
             nc.vector.memset(window[:, S:], 0.0)
         z = [keep.tile([P, HALF, PACK], BF16, name=f"z{c}", align_bytes=64) for c in range(2)]
 
@@ -109,23 +115,27 @@ def tile_picked_hcodeswapdpagmx_none_p_kernel(
             nc.scalar.activation(pa[t][:], h[t][:].indirect(n1_l[:]), COPY)
             nc.vector.tensor_tensor(rb[t][:], pa[t][:], pb[t][:], ALU.subtract)
 
-        def weigh(t, c, far):
+        halves = [slice(0, HALF), slice(HALF, S)]
+
+        def take_larger(t, c, far):
             top = keep.tile([P, HALF], F32, name=f"top{t}_{c}")
-            nc.vector.scalar_tensor_tensor(
-                top[:], far, 0.5, dt[t][:, HALF * c : HALF * (c + 1)], ALU.mult, ALU.max
-            )
+            nc.vector.scalar_tensor_tensor(top[:], far, 0.5, dt[t][:, halves[c]], ALU.mult, ALU.max)
+            return top
+
+        def weigh(t, c, top):
             nc.vector.tensor_scalar(z[c][:, :, t], top[:], gain[:, t : t + 1], None, ALU.mult)
 
         def fetch_partners(t):
             far = keep.tile([P, S], F32, name=f"far{t}")
             nc.scalar.activation(far[:], dt[t][:].indirect(n3_l[:]), COPY)
+            tops = [take_larger(t, c, far[:, halves[c]]) for c in range(2)]
             for c in range(2):
-                weigh(t, c, far[:, HALF * c : HALF * (c + 1)])
+                weigh(t, c, tops[c])
 
         def fetch_half_partners(t, c):
             far = keep.tile([P, HALF], F32, name=f"far{t}_{c}")
             nc.scalar.activation(far[:], dt[t][:].indirect(n3_l[:, 8 * c : 8 * c + 8]), COPY)
-            weigh(t, c, far[:])
+            return take_larger(t, c, far[:])
 
         fetch_pairs(0)
         for t in range(PACK):
@@ -140,7 +150,7 @@ def tile_picked_hcodeswapdpagmx_none_p_kernel(
                 nc.vector.tensor_copy(w2_bytes[:], d_sc[:].indirect(k2_l[:]))
                 plane2 = keep.tile([P, H], U8, name="plane2", align_bytes=64)
                 nc.vector.tensor_copy(plane2[:].bitcast(I32), w2_bytes[:].bitcast(I32))
-                place_scale_rows(plane2, nc.sync)
+                place_scale_rows(plane2, (nc.sync, nc.sync, nc.sync))
             if t == 1:
                 w2 = keep.tile([P, H], U32, name="w2", tag="after_pairs1", align_bytes=64)
                 nc.vector.tensor_copy(w2[:], d_w[:].indirect(k2_l[:]))
@@ -161,13 +171,17 @@ def tile_picked_hcodeswapdpagmx_none_p_kernel(
             else:
                 nc.vector.tensor_scalar(h2[u][:, cols], acc[:], 0.0625, None, ALU.mult)
 
+        last = [(3, 0), (3, 1)]
+        tops = [fetch_half_partners(t, c) for t, c in last]
+        for (t, c), top in zip(last, tops):
+            weigh(t, c, top)
         for c in range(2):
-            cols = slice(HALF * c, HALF * (c + 1))
-            fetch_half_partners(PACK - 1, c)
             nc.vector.quantize_mx(
-                out=zq[:, cols].bitcast(FP8X4), scales=zq_sc[:, cols], in_=z[c][:].rearrange("p j t -> p (j t)")
+                out=zq[:, halves[c]].bitcast(FP8X4), scales=zq_sc[:, halves[c]],
+                in_=z[c][:].rearrange("p j t -> p (j t)"),
             )
-            second_product(0, cols, 4 + c, c == 0)
+        for c in range(2):
+            second_product(0, halves[c], 5 + c, c == 0)
         for u in range(1, PACK):
             second_product(u, slice(0, S), u, False)
 

@@ -85,18 +85,12 @@ def tile_picked_hcodeswapdpagmx_none_p_kernel(
             w1 = keep.tile([P, P], U32, name=f"w1_{t}", align_bytes=64)
             nc.vector.tensor_copy(w1[:], w1_picked[:, t:H:PACK])
             h_t = keep.tile([P, S], F32, name=f"h{t}")
-            parts = [(slice(0, HALF), 4), (slice(HALF, S), 0)] if t == 0 else [(slice(0, S), t)]
-            for cols, bank in parts:
-                acc = psum.tile([P, cols.stop - cols.start], F32, name=f"acc1_{bank}", tag=f"bank{bank}")
-                nc.tensor.matmul_mx(
-                    out=acc[:], lhsT=w1[:].bitcast(FP8X4), lhsT_scale=plane1[:, P * t : P * (t + 1)],
-                    rhs=xq[:, cols].bitcast(FP8X4), rhs_scale=plane1[:, H + cols.start : H + cols.stop],
-                    start=True, stop=True,
-                )
-                if bank == 4:
-                    nc.scalar.activation(h_t[:, cols], acc[:], COPY, scale=0.0625)
-                else:
-                    nc.vector.tensor_scalar(h_t[:, cols], acc[:], 0.0625, None, ALU.mult)
+            acc = psum.tile([P, S], F32, name=f"acc1_{t}", tag=f"bank{t}")
+            nc.tensor.matmul_mx(
+                out=acc[:], lhsT=w1[:].bitcast(FP8X4), lhsT_scale=plane1[:, P * t : P * (t + 1)],
+                rhs=xq[:].bitcast(FP8X4), rhs_scale=plane1[:, H:], start=True, stop=True,
+            )
+            nc.vector.tensor_scalar(h_t[:], acc[:], 0.0625, None, ALU.mult)
             h.append(h_t)
 
         gain = keep.tile([P, PACK], F32, name="gain", tag="after_deal", align_bytes=64)
@@ -140,11 +134,10 @@ def tile_picked_hcodeswapdpagmx_none_p_kernel(
         fetch_pairs(0)
         for t in range(PACK):
             nc.scalar.activation(dt[t][:].indirect(n1_l[:]), pb[t][:], COPY)
-            if t > 0:
-                fetch_partners(t - 1)
             nc.scalar.activation(dt[t][:].indirect(n2_l[:]), rb[t][:], COPY)
             if t + 1 < PACK:
                 fetch_pairs(t + 1)
+                fetch_partners(t)
             if t == 0:
                 w2_bytes = keep.tile([P, H], U8, name="w2_bytes", tag="after_pairs0", align_bytes=64)
                 nc.vector.tensor_copy(w2_bytes[:], d_sc[:].indirect(k2_l[:]))
@@ -181,8 +174,9 @@ def tile_picked_hcodeswapdpagmx_none_p_kernel(
                 in_=z[c][:].rearrange("p j t -> p (j t)"),
             )
         for c in range(2):
-            second_product(0, halves[c], 5 + c, c == 0)
-        for u in range(1, PACK):
+            for u in range(2):
+                second_product(u, halves[c], 4 + 2 * c + u, c == 0)
+        for u in range(2, PACK):
             second_product(u, slice(0, S), u, False)
 
         up = [keep.tile([P, S], F32, name=f"up{u}") for u in range(PACK)]

from contextlib import ExitStack

import concourse.mybir as mybir

K, T, S, G, H, W, U = 512, 1024, 256, 2048, 512, 128, 512
FLOPS = 2 * 2 * K * H * S

F32 = mybir.dt.float32
BF16 = mybir.dt.bfloat16
I32 = mybir.dt.int32
U32 = mybir.dt.uint32
U16 = mybir.dt.uint16
U8 = mybir.dt.uint8
FP8X4 = mybir.dt.float8_e4m3fn_x4
ALU = mybir.AluOpType
COPY = mybir.ActivationFunctionType.Copy

P = 128
PACK = 4
HALF = S // 2
SPARE = 16


def tile_picked_hcodeswapdpagmx_none_p_kernel(
    tc, x_words, x_scales, d_words, d_scales, gs, offs, k1, n1, n2, n3, k2, n4, n5, n6, out
):
    nc = tc.nc
    with ExitStack() as ctx:
        lists = ctx.enter_context(tc.tile_pool(name="lists", bufs=1))
        keep = ctx.enter_context(tc.tile_pool(name="keep", bufs=1))
        psum = ctx.enter_context(tc.psum_pool(name="psum", bufs=1))

        def load_list(name, src):
            held = lists.tile(list(src.shape), U16, name=name)
            nc.sync.dma_start(held[:], src)
            return held

        def load_scale_rows(name, src, width, clear):
            window = keep.tile([P, width], U8, name=name, align_bytes=64)
            clear.memset(window[:].bitcast(I32), 0)
            nc.sync.dma_start(window[0:P:8, :].bitcast(I32), src[0].bitcast(I32))
            return window

        def load_words(name, src, width):
            window = keep.tile([P, width], U32, name=name, align_bytes=64)
            nc.sync.dma_start(window[:].bitcast(I32), src[0].rearrange("p n r -> p (n r)").bitcast(I32))
            return window

        def place_scale_rows(plane, queues):
            for a, queue in zip(range(1, 4), queues):
                queue.dma_start(plane[a:P:32, :].bitcast(I32), plane[8 * a : P : 32, :].bitcast(I32))

        k1_l = load_list("k1_l", k1)
        offs_l = load_list("offs_l", offs)
        d_sc = load_scale_rows("d_sc", d_scales, G, nc.gpsimd)
        x_sc = load_scale_rows("x_sc", x_scales, T, nc.vector)
        d_w = load_words("d_w", d_words, G)
        n2_l = load_list("n2_l", n2)
        n1_l = load_list("n1_l", n1)
        n3_l = load_list("n3_l", n3)
        x_w = load_words("x_w", x_words, T)
        k2_l = load_list("k2_l", k2)
        n6_l = load_list("n6_l", n6)
        n4_l = load_list("n4_l", n4)
        n5_l = load_list("n5_l", n5)

        plane1 = keep.tile([P, H + S], U8, name="plane1", align_bytes=64)
        w1_bytes = keep.tile([P, H], U8, name="w1_bytes", align_bytes=64)
        nc.vector.tensor_copy(w1_bytes[:], d_sc[:].indirect(k1_l[:]))
        nc.vector.tensor_copy(
            plane1[:, 0:H].rearrange("p (t m) -> p t m", t=PACK), w1_bytes[:].rearrange("p (m t) -> p t m", t=PACK)
        )
        xq_bytes = keep.tile([P, S], U8, name="xq_bytes", align_bytes=64)
        nc.vector.tensor_copy(xq_bytes[:], x_sc[:].indirect(offs_l[:]))
        nc.vector.tensor_copy(plane1[:, H:].bitcast(I32), xq_bytes[:].bitcast(I32))
        place_scale_rows(plane1, (nc.scalar, nc.scalar, nc.scalar))

        w1_picked = keep.tile([P, H], U32, name="w1_picked", tag="after_deal", align_bytes=64)
        nc.vector.tensor_copy(w1_picked[:], d_w[:].indirect(k1_l[:]))
        xq = keep.tile([P, S], U32, name="xq", align_bytes=64)
        nc.vector.tensor_copy(xq[:], x_w[:].indirect(offs_l[:]))

        h = []
        for t in range(PACK):
            w1 = keep.tile([P, P], U32, name=f"w1_{t}", align_bytes=64)
            nc.vector.tensor_copy(w1[:], w1_picked[:, t:H:PACK])
            h_t = keep.tile([P, S], F32, name=f"h{t}")
            acc = psum.tile([P, S], F32, name=f"acc1_{t}", tag=f"bank{t}")
            nc.tensor.matmul_mx(
                out=acc[:], lhsT=w1[:].bitcast(FP8X4), lhsT_scale=plane1[:, P * t : P * (t + 1)],
                rhs=xq[:].bitcast(FP8X4), rhs_scale=plane1[:, H:], start=True, stop=True,
            )
            nc.vector.tensor_scalar(h_t[:], acc[:], 0.0625, None, ALU.mult)
            h.append(h_t)

        gain = keep.tile([P, PACK], F32, name="gain", tag="after_deal", align_bytes=64)
        nc.sync.dma_start(gain[:], gs.rearrange("k o -> (k o)").rearrange("(p t) -> p t", t=PACK))
        pa = [keep.tile([P, W], F32, name=f"pa{t}", tag=f"after_pairs{t}", align_bytes=64) for t in range(PACK)]
        pb = [keep.tile([P, W], F32, name=f"pb{t}") for t in range(PACK)]
        rb = [keep.tile([P, W], F32, name=f"rb{t}") for t in range(PACK)]
        dt = [keep.tile([P, S + (SPARE if t < 3 else 0)], F32, name=f"dt{t}") for t in range(PACK)]
        h2 = [keep.tile([P, S + SPARE], F32, name=f"h2_{u}") for u in range(PACK)]
        for window in dt[:3] + h2:
            nc.vector.memset(window[:, S:], 0.0)
        z = [keep.tile([P, HALF, PACK], BF16, name=f"z{c}", align_bytes=64) for c in range(2)]

        def fetch_pairs(t):
            nc.scalar.activation(pb[t][:], h[t][:].indirect(n2_l[:]), COPY)
            nc.scalar.activation(pa[t][:], h[t][:].indirect(n1_l[:]), COPY)
            nc.vector.tensor_tensor(rb[t][:], pa[t][:], pb[t][:], ALU.subtract)

        halves = [slice(0, HALF), slice(HALF, S)]

        def take_larger(t, c, far):
            top = keep.tile([P, HALF], F32, name=f"top{t}_{c}")
            nc.vector.scalar_tensor_tensor(top[:], far, 0.5, dt[t][:, halves[c]], ALU.mult, ALU.max)
            return top

        def weigh(t, c, top):
            nc.vector.tensor_scalar(z[c][:, :, t], top[:], gain[:, t : t + 1], None, ALU.mult)

        def fetch_partners(t):
            far = keep.tile([P, S], F32, name=f"far{t}")
            nc.scalar.activation(far[:], dt[t][:].indirect(n3_l[:]), COPY)
            tops = [take_larger(t, c, far[:, halves[c]]) for c in range(2)]
            for c in range(2):
                weigh(t, c, tops[c])

        def fetch_half_partners(t, c):
            far = keep.tile([P, HALF], F32, name=f"far{t}_{c}")
            nc.scalar.activation(far[:], dt[t][:].indirect(n3_l[:, 8 * c : 8 * c + 8]), COPY)
            return take_larger(t, c, far[:])

        fetch_pairs(0)
        for t in range(PACK):
            nc.scalar.activation(dt[t][:].indirect(n1_l[:]), pb[t][:], COPY)
            nc.scalar.activation(dt[t][:].indirect(n2_l[:]), rb[t][:], COPY)
            if t + 1 < PACK:
                fetch_pairs(t + 1)
                fetch_partners(t)
            if t == 0:
                w2_bytes = keep.tile([P, H], U8, name="w2_bytes", tag="after_pairs0", align_bytes=64)
                nc.vector.tensor_copy(w2_bytes[:], d_sc[:].indirect(k2_l[:]))
                plane2 = keep.tile([P, H], U8, name="plane2", align_bytes=64)
                nc.vector.tensor_copy(plane2[:].bitcast(I32), w2_bytes[:].bitcast(I32))
                place_scale_rows(plane2, (nc.sync, nc.sync, nc.sync))
            if t == 1:
                w2 = keep.tile([P, H], U32, name="w2", tag="after_pairs1", align_bytes=64)
                nc.vector.tensor_copy(w2[:], d_w[:].indirect(k2_l[:]))

        zq = keep.tile([P, S], U32, name="zq", align_bytes=64)
        zq_sc = keep.tile([P, S], U8, name="zq_sc", align_bytes=64)
        nc.vector.memset(zq_sc[:].bitcast(I32), 0)

        def second_product(u, cols, bank, copy_on_scalar):
            acc = psum.tile([P, cols.stop - cols.start], F32, name=f"acc2_{bank}", tag=f"bank{bank}")
            nc.tensor.matmul_mx(
                out=acc[:], lhsT=w2[:, P * u : P * (u + 1)].bitcast(FP8X4),
                lhsT_scale=plane2[:, P * u : P * (u + 1)],
                rhs=zq[:, cols].bitcast(FP8X4), rhs_scale=zq_sc[:, cols], start=True, stop=True,
            )
            if copy_on_scalar:
                nc.scalar.activation(h2[u][:, cols], acc[:], COPY, scale=0.0625)
            else:
                nc.vector.tensor_scalar(h2[u][:, cols], acc[:], 0.0625, None, ALU.mult)

        last = [(3, 0), (3, 1)]
        tops = [fetch_half_partners(t, c) for t, c in last]
        for (t, c), top in zip(last, tops):
            weigh(t, c, top)
        for c in range(2):
            nc.vector.quantize_mx(
                out=zq[:, halves[c]].bitcast(FP8X4), scales=zq_sc[:, halves[c]],
                in_=z[c][:].rearrange("p j t -> p (j t)"),
            )
        for c in range(2):
            for u in range(2):
                second_product(u, halves[c], 4 + 2 * c + u, c == 0)
        for u in range(2, PACK):
            second_product(u, slice(0, S), u, False)

        up = [keep.tile([P, S], F32, name=f"up{u}") for u in range(PACK)]
        dn = [keep.tile([P, S], F32, name=f"dn{u}") for u in range(PACK)]
        page = [keep.tile([P, U], F32, name=f"page{u}") for u in range(PACK)]

        def sort_pairs(u):
            mate = keep.tile([P, S], F32, name=f"mate{u}")
            nc.scalar.activation(mate[:], h2[u][:].indirect(n6_l[:]), COPY)
            nc.vector.tensor_tensor(up[u][:], h2[u][:, 0:S], mate[:], ALU.max)
            nc.vector.tensor_tensor(dn[u][:], h2[u][:, 0:S], mate[:], ALU.min)

        def put_up(u):
            nc.scalar.activation(page[u][:].indirect(n4_l[:]), up[u][:], COPY)

        def put_down(u):
            nc.scalar.activation(page[u][:].indirect(n5_l[:]), dn[u][:], COPY)
            nc.sync.dma_start(out[P * u : P * (u + 1), :], page[u][:])

        sort_pairs(0)
        sort_pairs(1)
        put_up(0)
        sort_pairs(2)
        put_down(0)
        put_up(1)
        sort_pairs(3)
        put_down(1)
        put_up(2)
        put_up(3)
        put_down(2)
        put_down(3)
